import numpy as np
import ml_dtypes


def mxq(x, axis, fmt="e4m3"):
    dtype, down = {"e4m3": (ml_dtypes.float8_e4m3fn, 7), "e5m2": (ml_dtypes.float8_e5m2, 14)}[fmt]
    v = np.moveaxis(np.asarray(x, np.float32).astype(ml_dtypes.bfloat16).astype(np.float64), axis, -1)
    blocks = v.reshape(v.shape[:-1] + (-1, 32))
    amax = np.abs(blocks).max(-1, keepdims=True)
    byte = np.maximum(np.where(amax > 0, np.frexp(amax)[1] - 1 + 127, 0) - down, 1)
    scale = np.exp2(byte - 127.0)
    codes = (blocks / scale).astype(np.float32).astype(dtype).astype(np.float64)
    return np.moveaxis((codes * scale).reshape(v.shape), -1, axis)


WIDE = False


def mx_kscale(k):
    if not WIDE:
        return np.ones(k)
    levels = np.array([10, -10, 5, -5, 0])
    if k % 512:
        return np.exp2(np.random.permutation(np.resize(levels, k // 32))).repeat(32)
    a = np.empty((k // 512, 16))
    for p in range(k // 512):
        a[p, :8] = np.random.permutation(np.resize(levels, 8))
        for g in range(8):
            far = levels[np.abs(levels - a[p, g]) >= 10]
            a[p, g + 8] = far[np.random.randint(len(far))]
    return np.exp2(a.ravel()).repeat(32)


def f64(x):
    return np.asarray(x).astype(np.float64)


def striped(idx):
    return np.tile(idx.reshape(-1, 16).T, (8, 1)).astype(np.uint16)


def unstriped(offs):
    return offs[:16].T.reshape(-1).astype(np.int64)


def striped8(idx):
    return np.concatenate([x.reshape(-1, 16).T for x in idx]).astype(np.uint16)


def runs(offs, k):
    lists = np.stack([offs[16 * r : 16 * r + 16].T.reshape(-1) for r in range(8)]).astype(np.int64)
    return lists[np.arange(k) % 512 // 64]


def pack_weight(w):
    k, n = w.shape
    w = f64(np.asarray(w, np.float32).astype(ml_dtypes.bfloat16)).reshape(k // 32, 32, n)
    amax = np.abs(w).max(1)
    byte = np.clip(np.where(amax > 0, np.frexp(amax)[1] - 1 + 127 - 7, 1), 1, 254)
    scaled = (w * np.exp2(127.0 - byte)[:, None, :]).reshape(k, n).astype(np.float32)
    words = np.ascontiguousarray(scaled.reshape(k // 512, 128, 4, n).transpose(0, 1, 3, 2)).astype(ml_dtypes.float8_e4m3fn).view(np.uint8)
    return words, np.ascontiguousarray(byte.astype(np.uint8).reshape(k // 512, 16, n))


def unpack_weight(words, scales):
    g, p, n, _ = words.shape
    vals = np.ascontiguousarray(words).view(ml_dtypes.float8_e4m3fn).astype(np.float64) * np.repeat(np.exp2(scales.astype(np.float64) - 127.0), 8, axis=1)[..., None]
    return vals.transpose(0, 1, 3, 2).reshape(g * 512, n)


def sigmoid(v):
    return 1.0 / (1.0 + np.exp(-np.maximum(v, -700.0)))


K, T, S, N, G, H, W = 512, 1024, 256, 512, 2048, 512, 128


def setup_inputs():
    n = np.random.standard_normal
    s = mx_kscale(K)[:, None]
    u = mx_kscale(K)
    packed_xT = pack_weight(n((K, T)) * s)
    packed_dT = pack_weight(n((K, G)) / s)
    perm = np.random.permutation(S)
    perm2 = np.random.permutation(S)
    return {
        "x_words": packed_xT[0],
        "x_scales": packed_xT[1],
        "d_words": packed_dT[0],
        "d_scales": packed_dT[1],
        "gn": (np.random.uniform(0.5, 1.5, (H, 1)) * u[:, None]).astype(np.float32),
        "w1": (n((H, N)) / np.sqrt(H) / u[:, None]).astype(np.float32),
        "sl": np.random.uniform(1.0, 2.0, (N, 1)).astype(np.float32),
        "th": (0.5 * n((N, 1))).astype(np.float32),
        "offs": striped(np.random.permutation(T)[:S]),
        "k1": striped8(np.random.randint(0, G, (8, H))),
        "hz": striped8(np.random.randint(0, T, (8, S))),
        "k2": striped8(np.random.randint(0, G, (8, H))),
        "hy": striped8(np.random.randint(0, T, (8, S))),
        "k3": striped8(np.random.randint(0, G, (8, H))),
        "n1": striped(perm[:W]),
        "n2": striped(perm[W:]),
        "n3": striped(perm2[:W]),
        "n4": striped(perm2[W:]),
        "n5": striped(np.random.permutation(S)),
        "n6": striped(np.random.permutation(S)),
        "n7": striped(np.random.permutation(S)),
        "n8": striped(np.random.permutation(S)),
    }


def reference(x_words, x_scales, d_words, d_scales, gn, w1, sl, th, offs, k1, hz, k2, hy, k3, n1, n2, n3, n4, n5, n6, n7, n8):
    d_k1 = unpack_weight(d_words, d_scales)[np.arange(K)[:, None], runs(k1, K)]
    xq = unpack_weight(x_words, x_scales)[:, unstriped(offs)]
    d_k2 = unpack_weight(d_words, d_scales)[np.arange(K)[:, None], runs(k2, K)]
    x_hz = unpack_weight(x_words, x_scales)[np.arange(K)[:, None], runs(hz, K)]
    d_k3 = unpack_weight(d_words, d_scales)[np.arange(K)[:, None], runs(k3, K)]
    x_hy = unpack_weight(x_words, x_scales)[np.arange(K)[:, None], runs(hy, K)]
    h = 0.0625 * (d_k1.T @ xq + d_k2.T @ x_hz + d_k3.T @ x_hy)
    pa = h[:, unstriped(n1)]
    pb = h[:, unstriped(n2)]
    rb = pa + pb
    ra = np.minimum(pa, pb)
    ua = np.zeros((H, S))
    ua[:, unstriped(n3)] = ra
    ub = ua.copy()
    ub[:, unstriped(n4)] = rb
    ds = np.zeros((H, S))
    ds[:, unstriped(n5)] = ub
    z = f64(gn) * (ub - ds)
    h2 = mxq(f64(w1), 0, "e4m3").T @ mxq(z, 0, "e4m3")
    ds3 = np.zeros((N, S))
    ds3[:, unstriped(n7)] = h2
    ds2 = np.zeros((N, S))
    ds2[:, unstriped(n6)] = h2
    sg = sigmoid(f64(sl) * (ds2[:, unstriped(n8)] - f64(th)))
    return ds3 * sg

@@ -1,0 +1,317 @@
+import concourse.mybir as mybir
+
+F32 = mybir.dt.float32
+BF16 = mybir.dt.bfloat16
+I32 = mybir.dt.int32
+U32 = mybir.dt.uint32
+U16 = mybir.dt.uint16
+U8 = mybir.dt.uint8
+FP8X4 = mybir.dt.float8_e4m3fn_x4
+ACT = mybir.ActivationFunctionType
+ALU = mybir.AluOpType
+
+P = 128
+T, G, S, H, N, W = 1024, 2048, 256, 512, 512, 128
+HALF = H // 2
+WIDE = 2 * S
+FLOPS = 2 * 512 * H * S * 3 + 2 * H * N * S
+
+
+def tile_picked_mthhzncpsdesntw_none_p_kernel(
+    tc, x_words, x_scales, d_words, d_scales, gn, w1, sl, th,
+    offs, k1, hz, k2, hy, k3, n1, n2, n3, n4, n5, n6, n7, n8, out,
+):
+    nc = tc.nc
+    with (
+        tc.tile_pool(name="lists", bufs=1) as lists,
+        tc.tile_pool(name="sb", bufs=1) as sb,
+        tc.psum_pool(name="psum", bufs=1) as psum,
+    ):
+        def tile(shape, dtype, name, tag=None):
+            return sb.tile(shape, dtype, name=name, tag=tag or name, align_bytes=64)
+
+        def load_list(ap, name):
+            t = lists.tile(list(ap.shape), U16, name=name)
+            nc.sync.dma_start(t[:], ap)
+            return t
+
+        def load_scales(ap, cols, name):
+            t = tile([P, cols], U8, name)
+            rows = ap[0].bitcast(I32).unsqueeze(1).to_broadcast([16, 8, cols // 4])
+            nc.scalar.dma_start(t[:].bitcast(I32), rows)
+            return t
+
+        def load_words(ap, cols, name):
+            t = tile([P, cols], I32, name)
+            nc.scalar.dma_start(t[:], ap[0].rearrange("p n t -> p (n t)").bitcast(I32))
+            return t
+
+        ds_tab = load_scales(d_scales, G, "ds_tab")
+        d_lists = [load_list(k1, "k1"), load_list(k2, "k2"), load_list(k3, "k3")]
+        xs_tab = load_scales(x_scales, T, "xs_tab")
+        x_lists = [load_list(offs, "offs"), load_list(hz, "hz"), load_list(hy, "hy")]
+        xw_tab = load_words(x_words, T, "xw_tab")
+        dw_tab = load_words(d_words, G, "dw_tab")
+
+        first_plane = tile([P, 3 * P + 3 * S], U8, "first_plane")
+        a_plane = first_plane[:, : 3 * P]
+        x_plane = first_plane[:, 3 * P :]
+        r_plane = tile([P, 3 * 3 * P], U8, "r_plane")
+        for plane in (first_plane, r_plane):
+            nc.vector.memset(plane[:].bitcast(I32), 0)
+
+        def place_rows(plane, gathered):
+            for r in range(4):
+                nc.sync.dma_start(plane[r:P:32, :].bitcast(I32), gathered[8 * r : P : 32, :].bitcast(I32))
+
+        def half_of(lst, half):
+            return lst[:, half * HALF // 16 : (half + 1) * HALF // 16]
+
+        def gather_d_bytes(half, tag):
+            t = tile([P, 3 * HALF], U8, "d_bytes%d" % half, tag)
+            for l in range(3):
+                nc.vector.tensor_copy(t[:, l * HALF : (l + 1) * HALF], ds_tab[:].indirect(half_of(d_lists[l], half)))
+            return t[:].bitcast(I32).rearrange("p (l b s r) -> p l s b r", l=3, b=8, s=4)
+
+        def gather_d_words(l, half, tag):
+            t = tile([P, HALF], I32, "d_words%d_%d" % (half, l), tag)
+            nc.vector.tensor_copy(t[:].bitcast(U32), dw_tab[:].bitcast(U32).indirect(half_of(d_lists[l], half)))
+            return t[:].rearrange("p (b s r) -> p s b r", b=8, s=4)
+
+        d_bytes0 = gather_d_bytes(0, None)
+        first_bytes = tile([P, 3 * P + 3 * S], U8, "first_bytes")
+        nc.vector.tensor_copy(
+            first_bytes[:, : 3 * P].bitcast(I32).rearrange("p (l s b r) -> p l s b r", l=3, s=2, b=8), d_bytes0[:, :, 0:2]
+        )
+        x_bytes = tile([P, 3 * S], U8, "x_bytes")
+        for l in range(3):
+            nc.vector.tensor_copy(x_bytes[:, l * S : (l + 1) * S], xs_tab[:].indirect(x_lists[l][:]))
+        nc.vector.tensor_copy(first_bytes[:, 3 * P :].bitcast(I32), x_bytes[:].bitcast(I32))
+        place_rows(first_plane, first_bytes)
+        l1, l2, l3, l4, l5, l6, l7, l8 = [
+            load_list(ap, "n%d" % (i + 1)) for i, ap in enumerate((n1, n2, n3, n4, n5, n6, n7, n8))
+        ]
+
+        cols = tile([P, 6, 8], F32, "cols", "x_bytes")
+        gn_rows = gn.rearrange("(b s r) o -> s b r o", s=4, r=8)
+        with nc.allow_non_contiguous_dma(reason="one value a partition"):
+            for s in range(4):
+                nc.sync.dma_start(cols[:, s, 0:1], gn_rows[s])
+            nc.sync.dma_start(cols[:, 4, 0:4], sl.rearrange("(m p) o -> p (m o)", p=P))
+            nc.sync.dma_start(cols[:, 5, 0:4], th.rearrange("(m p) o -> p (m o)", p=P))
+        prod = tile([P, 4], F32, "prod")
+        bias = tile([P, 4], F32, "bias")
+        nc.gpsimd.tensor_tensor(prod[:], cols[:, 4, 0:4], cols[:, 5, 0:4], ALU.mult)
+        nc.gpsimd.tensor_scalar(bias[:], prod[:], -1.0, None, ALU.mult)
+        neg_gain = tile([P, 1], F32, "neg_gain")
+        nc.gpsimd.tensor_scalar(neg_gain[:], cols[:, 3, 0:1], -1.0, None, ALU.mult)
+        w_raw = tile([P, 4, N], F32, "w_raw", "first_bytes")
+        w_rows = w1.rearrange("(b s r) n -> s b r n", s=4, r=8)
+        for s in range(4):
+            nc.sync.dma_start(w_raw[:, s, :], w_rows[s])
+
+        x_codes = []
+        for l in range(3):
+            t = tile([P, S], I32, "x_codes%d" % l)
+            nc.vector.tensor_copy(t[:].bitcast(U32), xw_tab[:].bitcast(U32).indirect(x_lists[l][:]))
+            x_codes.append(t)
+
+        def deal_pair(src, name):
+            t = tile([P, P], I32, name)
+            nc.vector.tensor_copy(t[:].rearrange("p (s b r) -> p s b r", s=2, b=8), src[:, 0:2])
+            return t
+
+        def deal_cd(src, l, half):
+            dst = cd_codes[:, l, :, 64 * half : 64 * (half + 1)].rearrange("p s (b r) -> p s b r", b=8)
+            nc.vector.tensor_copy(dst, src[:, 2:4])
+
+        def product(codes, scales, name):
+            acc = psum.tile([P, S], F32, name=name)
+            for l in range(3):
+                nc.tensor.matmul_mx(
+                    acc[:], lhsT=codes[l].bitcast(FP8X4), lhsT_scale=scales[l],
+                    rhs=x_codes[l][:].bitcast(FP8X4), rhs_scale=x_plane[:, l * S : (l + 1) * S],
+                    start=(l == 0), stop=(l == 2),
+                )
+            return acc
+
+        words0 = [gather_d_words(l, 0, None) for l in range(2)]
+        a_codes = [deal_pair(words0[0], "a_codes0")]
+        words0.append(gather_d_words(2, 0, None))
+        a_codes.extend(deal_pair(words0[l], "a_codes%d" % l) for l in (1, 2))
+        acc_a = product([t[:] for t in a_codes], [a_plane[:, l * P : (l + 1) * P] for l in range(3)], "acc_a")
+
+        def fetch_pairs(h, name):
+            pa = tile([P, W], F32, "pa_" + name)
+            pb = tile([P, W], F32, "pb_" + name)
+            nc.scalar.activation(pa[:], h[:].indirect(l1[:]), ACT.Copy)
+            nc.scalar.activation(pb[:], h[:].indirect(l2[:]), ACT.Copy)
+            return pa, pb
+
+        def combine(pair, name):
+            pa, pb = pair
+            ra = tile([P, W], F32, "ra_" + name)
+            rb = tile([P, W], F32, "rb_" + name)
+            nc.vector.tensor_tensor(ra[:], pa[:], pb[:], ALU.min)
+            nc.vector.tensor_tensor(rb[:], pa[:], pb[:], ALU.add)
+            return ra, rb
+
+        def put(window, lst, values):
+            nc.scalar.activation(window[:].indirect(lst), values, ACT.Copy)
+
+        h_a = tile([P, S], F32, "h_a")
+        nc.scalar.activation(h_a[:], acc_a[:], ACT.Copy, scale=0.0625)
+        pair_a = fetch_pairs(h_a, "a")
+
+        d_bytes1 = gather_d_bytes(1, "a_codes0")
+        res = {"a": combine(pair_a, "a")}
+        r_bytes = tile([P, 3 * 3 * P], U8, "r_bytes", "pb_a")
+        r_view = r_bytes[:].bitcast(I32).rearrange("p (l t h b r) -> p l t h b r", l=3, t=3, h=2, b=8)
+        nc.vector.tensor_copy(r_view[:, :, 0], d_bytes1[:, :, 0:2])
+        nc.vector.tensor_copy(r_view[:, :, 1:3, 0], d_bytes0[:, :, 2:4])
+        nc.vector.tensor_copy(r_view[:, :, 1:3, 1], d_bytes1[:, :, 2:4])
+        place_rows(r_plane, r_bytes)
+
+        ub = {}
+        ds = {}
+        for name in "abcd":
+            ub[name] = tile([P, S], F32, "ub_" + name)
+            ds[name] = tile([P, WIDE], F32, "ds_" + name)
+
+        def put3(name):
+            put(ub[name], l3[:], res[name][0][:])
+
+        def put4(name):
+            put(ub[name], l4[:], res[name][1][:])
+
+        def put5(name):
+            put(ds[name], l5[:], ub[name][:])
+
+        put3("a")
+        put4("a")
+        put5("a")
+
+        words1 = [gather_d_words(l, 1, tag) for l, tag in enumerate(("pa_a", "a_codes0"))]
+        b_codes = [deal_pair(words1[0], "b_codes0")]
+        words1.append(gather_d_words(2, 1, "ra_a"))
+        b_codes.extend(deal_pair(words1[l], "b_codes%d" % l) for l in (1, 2))
+
+        def r_scales(t):
+            return [r_plane[:, (3 * l + t) * P : (3 * l + t + 1) * P] for l in range(3)]
+
+        def scaled(acc, name):
+            h = tile([P, S], F32, "h_" + name)
+            nc.vector.tensor_scalar(h[:], acc[:], 0.0625, None, ALU.mult)
+            return h
+
+        acc_b = product([t[:] for t in b_codes], r_scales(0), "acc_b")
+        h_b = tile([P, S], F32, "h_b")
+        nc.scalar.activation(h_b[:], acc_b[:], ACT.Copy, scale=0.0625)
+        pair_b = fetch_pairs(h_b, "b")
+        cd_codes = tile([P, 3, 2, P], I32, "cd_codes", "b_codes0")
+        for l in range(3):
+            deal_cd(words0[l], l, 0)
+            deal_cd(words1[l], l, 1)
+        res["b"] = combine(pair_b, "b")
+        h_c = scaled(product([cd_codes[:, l, 0, :] for l in range(3)], r_scales(1), "acc_c"), "c")
+        h_d = scaled(product([cd_codes[:, l, 1, :] for l in range(3)], r_scales(2), "acc_d"), "d")
+        put3("b")
+        pair_c = fetch_pairs(h_c, "c")
+        put4("b")
+        pair_d = fetch_pairs(h_d, "d")
+        res["c"] = combine(pair_c, "c")
+        res["d"] = combine(pair_d, "d")
+        put5("b")
+        put3("c")
+        put3("d")
+        put4("c")
+        put4("d")
+        put5("c")
+        put5("d")
+
+        z = tile([P, 4 * S], BF16, "z")
+        z_slots = z[:].rearrange("p (j s) -> p j s", s=4)
+
+        def difference(name, tag, j0, j1):
+            d = tile([P, j1 - j0], F32, "diff_%s%d" % (name, j0), tag)
+            nc.vector.tensor_tensor(d[:], ub[name][:, j0:j1], ds[name][:, j0:j1], ALU.subtract)
+            return d
+
+        def gain(d, s, j0, j1):
+            nc.vector.tensor_scalar(z_slots[:, j0:j1, s], d[:], cols[:, s, 0:1], None, ALU.mult)
+
+        slot0 = difference("a", "h_c", 0, S)
+        slot1 = tile([P, S], F32, "slot1")
+        nc.sync.dma_start(slot1[0:64, :], slot0[64:P, :])
+
+        w_codes = []
+        w_scales = []
+        for m, tag in enumerate(("pa_c", "pb_c", "pa_d", "h_d")):
+            w_bf = tile([P, 4 * P], BF16, "w_bf%d" % m, tag)
+            nc.vector.tensor_copy(
+                w_bf[:].rearrange("p (c i s) -> p c s i", i=4, s=4),
+                w_raw[:, :, m * P : (m + 1) * P].rearrange("p s (c i) -> p c s i", i=4),
+            )
+            codes = tile([P, P], I32, "w_codes%d" % m)
+            scales = tile([P, P], U8, "w_scales%d" % m)
+            nc.vector.quantize_mx(codes[:].bitcast(FP8X4), scales[:], w_bf[:])
+            w_codes.append(codes)
+            w_scales.append(scales)
+
+        diff_b = difference("b", "pb_d", 0, S)
+        nc.sync.dma_start(slot0[64:P, :], diff_b[0:64, :])
+        nc.sync.dma_start(slot1[64:P, :], diff_b[64:P, :])
+        gain(slot0, 0, 0, S)
+        gain(slot1, 1, 0, S)
+        gain(difference("c", None, 0, S), 2, 0, S)
+        gained = tile([P, S], F32, "gained")
+        nc.vector.tensor_scalar(gained[:], ub["d"][:], cols[:, 3, 0:1], None, ALU.mult)
+        z_codes = tile([P, S], I32, "z_codes")
+        z_scales = tile([P, S], U8, "z_scales")
+        first_pieces = [(0, 64), (64, W), (W, S)]
+        for j0, j1 in first_pieces:
+            nc.vector.scalar_tensor_tensor(
+                z_slots[:, j0:j1, 3], ds["d"][:, j0:j1], neg_gain[:], gained[:, j0:j1], ALU.mult, ALU.add
+            )
+            nc.vector.quantize_mx(z_codes[:, j0:j1].bitcast(FP8X4), z_scales[:, j0:j1], z[:, 4 * j0 : 4 * j1])
+
+        def dense(m, j0, j1, tag):
+            acc = psum.tile([P, j1 - j0], F32, name="acc2_%d_%d" % (m, j0), tag=tag)
+            nc.tensor.matmul_mx(
+                acc[:], lhsT=w_codes[m][:].bitcast(FP8X4), lhsT_scale=w_scales[m][:],
+                rhs=z_codes[:, j0:j1].bitcast(FP8X4), rhs_scale=z_scales[:, j0:j1], start=True, stop=True,
+            )
+            return acc
+
+        h2 = []
+        first = []
+        for u, (j0, j1) in enumerate(first_pieces):
+            t = tile([P, j1 - j0], F32, "h2_0_%d" % u)
+            acc = dense(0, j0, j1, ("acc_a", "acc_b", "acc2_0")[u])
+            if u == 0:
+                nc.scalar.copy(t[:], acc[:])
+            else:
+                nc.vector.tensor_copy(t[:], acc[:])
+            first.append((t, j0, j1))
+        h2.append(first)
+        for m in range(1, 4):
+            t = tile([P, S], F32, "h2_%d" % m)
+            nc.vector.tensor_copy(t[:], dense(m, 0, S, "acc2_%d" % m)[:])
+            h2.append([(t, 0, S)])
+
+        for m in range(4):
+            ds2 = tile([P, WIDE], F32, "ds2_%d" % m)
+            ds3 = tile([P, WIDE], F32, "ds3_%d" % m)
+            for t, j0, j1 in h2[m]:
+                put(ds2, l6[:, j0 // 16 : j1 // 16], t[:])
+                put(ds3, l7[:, j0 // 16 : j1 // 16], t[:])
+            pieces = [(0, W), (W, S)] if m == 3 else [(0, S)]
+            for j0, j1 in pieces:
+                sg = tile([P, j1 - j0], F32, "sg_%d_%d" % (m, j0))
+                nc.scalar.activation(
+                    sg[:], ds2[:].indirect(l8[:, j0 // 16 : j1 // 16]), ACT.Sigmoid,
+                    scale=cols[:, 4, m : m + 1], bias=bias[:, m : m + 1],
+                )
+                res_out = tile([P, j1 - j0], F32, "out_%d_%d" % (m, j0))
+                nc.vector.tensor_tensor(res_out[:], ds3[:, j0:j1], sg[:], ALU.mult)
+                nc.sync.dma_start(out[m * P : (m + 1) * P, j0:j1], res_out[:])

@@ -41,17 +41,21 @@ def tile_picked_mthhzncpsdesntw_none_p_kernel(
             nc.scalar.dma_start(t[:].bitcast(I32), rows)
             return t
 
-        def load_words(ap, cols, name):
+        def load_words(ap, cols, name, queue):
             t = tile([P, cols], I32, name)
-            nc.scalar.dma_start(t[:], ap[0].rearrange("p n t -> p (n t)").bitcast(I32))
+            queue.dma_start(t[:], ap[0].rearrange("p n t -> p (n t)").bitcast(I32))
             return t
 
+        xs_tab = load_scales(x_scales, T, "xs_tab")
+        x_lists = [load_list(offs, "offs")]
         ds_tab = load_scales(d_scales, G, "ds_tab")
         d_lists = [load_list(k1, "k1"), load_list(k2, "k2"), load_list(k3, "k3")]
-        xs_tab = load_scales(x_scales, T, "xs_tab")
-        x_lists = [load_list(offs, "offs"), load_list(hz, "hz"), load_list(hy, "hy")]
-        xw_tab = load_words(x_words, T, "xw_tab")
-        dw_tab = load_words(d_words, G, "dw_tab")
+        x_lists.extend([load_list(hz, "hz"), load_list(hy, "hy")])
+        dw_tab = load_words(d_words, G, "dw_tab", nc.sync)
+        xw_tab = load_words(x_words, T, "xw_tab", nc.sync)
+        l1, l2, l3, l4, l5, l6, l7, l8 = [
+            load_list(ap, "n%d" % (i + 1)) for i, ap in enumerate((n1, n2, n3, n4, n5, n6, n7, n8))
+        ]
 
         first_plane = tile([P, 3 * P + 3 * S], U8, "first_plane")
         a_plane = first_plane[:, : 3 * P]
@@ -78,21 +82,23 @@ def tile_picked_mthhzncpsdesntw_none_p_kernel(
             nc.vector.tensor_copy(t[:].bitcast(U32), dw_tab[:].bitcast(U32).indirect(half_of(d_lists[l], half)))
             return t[:].rearrange("p (b s r) -> p s b r", b=8, s=4)
 
+        x_bytes = tile([P, 3 * S], U8, "x_bytes")
+
+        def gather_x_bytes(l):
+            nc.vector.tensor_copy(x_bytes[:, l * S : (l + 1) * S], xs_tab[:].indirect(x_lists[l][:]))
+
+        gather_x_bytes(0)
         d_bytes0 = gather_d_bytes(0, None)
-        first_bytes = tile([P, 3 * P + 3 * S], U8, "first_bytes")
+        first_bytes = tile([P, 3 * P + 3 * S], U8, "first_bytes", "xs_tab")
+        gather_x_bytes(1)
+        gather_x_bytes(2)
         nc.vector.tensor_copy(
             first_bytes[:, : 3 * P].bitcast(I32).rearrange("p (l s b r) -> p l s b r", l=3, s=2, b=8), d_bytes0[:, :, 0:2]
         )
-        x_bytes = tile([P, 3 * S], U8, "x_bytes")
-        for l in range(3):
-            nc.vector.tensor_copy(x_bytes[:, l * S : (l + 1) * S], xs_tab[:].indirect(x_lists[l][:]))
         nc.vector.tensor_copy(first_bytes[:, 3 * P :].bitcast(I32), x_bytes[:].bitcast(I32))
         place_rows(first_plane, first_bytes)
-        l1, l2, l3, l4, l5, l6, l7, l8 = [
-            load_list(ap, "n%d" % (i + 1)) for i, ap in enumerate((n1, n2, n3, n4, n5, n6, n7, n8))
-        ]
 
-        cols = tile([P, 6, 8], F32, "cols", "x_bytes")
+        cols = tile([P, 6, 8], F32, "cols", "xs_tab")
         gn_rows = gn.rearrange("(b s r) o -> s b r o", s=4, r=8)
         with nc.allow_non_contiguous_dma(reason="one value a partition"):
             for s in range(4):
@@ -105,16 +111,7 @@ def tile_picked_mthhzncpsdesntw_none_p_kernel(
         nc.gpsimd.tensor_scalar(bias[:], prod[:], -1.0, None, ALU.mult)
         neg_gain = tile([P, 1], F32, "neg_gain")
         nc.gpsimd.tensor_scalar(neg_gain[:], cols[:, 3, 0:1], -1.0, None, ALU.mult)
-        w_raw = tile([P, 4, N], F32, "w_raw", "first_bytes")
-        w_rows = w1.rearrange("(b s r) n -> s b r n", s=4, r=8)
-        for s in range(4):
-            nc.sync.dma_start(w_raw[:, s, :], w_rows[s])
 
-        x_codes = []
-        for l in range(3):
-            t = tile([P, S], I32, "x_codes%d" % l)
-            nc.vector.tensor_copy(t[:].bitcast(U32), xw_tab[:].bitcast(U32).indirect(x_lists[l][:]))
-            x_codes.append(t)
 
         def deal_pair(src, name):
             t = tile([P, P], I32, name)
@@ -130,16 +127,26 @@ def tile_picked_mthhzncpsdesntw_none_p_kernel(
             for l in range(3):
                 nc.tensor.matmul_mx(
                     acc[:], lhsT=codes[l].bitcast(FP8X4), lhsT_scale=scales[l],
-                    rhs=x_codes[l][:].bitcast(FP8X4), rhs_scale=x_plane[:, l * S : (l + 1) * S],
+                    rhs=x_codes[:, l * S : (l + 1) * S].bitcast(FP8X4), rhs_scale=x_plane[:, l * S : (l + 1) * S],
                     start=(l == 0), stop=(l == 2),
                 )
             return acc
 
-        words0 = [gather_d_words(l, 0, None) for l in range(2)]
-        a_codes = [deal_pair(words0[0], "a_codes0")]
-        words0.append(gather_d_words(2, 0, None))
-        a_codes.extend(deal_pair(words0[l], "a_codes%d" % l) for l in (1, 2))
-        acc_a = product([t[:] for t in a_codes], [a_plane[:, l * P : (l + 1) * P] for l in range(3)], "acc_a")
+        d_words0 = tile([P, 3 * HALF], I32, "d_words0")
+        for l in range(3):
+            nc.vector.tensor_copy(
+                d_words0[:, l * HALF : (l + 1) * HALF].bitcast(U32),
+                dw_tab[:].bitcast(U32).indirect(half_of(d_lists[l], 0)),
+            )
+        words0 = d_words0[:].rearrange("p (l b s r) -> p s l b r", l=3, b=8, s=4)
+        a_codes = tile([P, 3 * P], I32, "a_codes")
+        nc.vector.tensor_copy(a_codes[:].rearrange("p (l s b r) -> p s l b r", l=3, s=2, b=8), words0[:, 0:2])
+        x_codes = tile([P, 3 * S], I32, "x_codes")
+        for l in range(3):
+            nc.vector.tensor_copy(
+                x_codes[:, l * S : (l + 1) * S].bitcast(U32), xw_tab[:].bitcast(U32).indirect(x_lists[l][:])
+            )
+        acc_a = product([a_codes[:, l * P : (l + 1) * P] for l in range(3)], [a_plane[:, l * P : (l + 1) * P] for l in range(3)], "acc_a")
 
         def fetch_pairs(h, name):
             pa = tile([P, W], F32, "pa_" + name)
@@ -163,7 +170,7 @@ def tile_picked_mthhzncpsdesntw_none_p_kernel(
         nc.scalar.activation(h_a[:], acc_a[:], ACT.Copy, scale=0.0625)
         pair_a = fetch_pairs(h_a, "a")
 
-        d_bytes1 = gather_d_bytes(1, "a_codes0")
+        d_bytes1 = gather_d_bytes(1, "xw_tab")
         res = {"a": combine(pair_a, "a")}
         r_bytes = tile([P, 3 * 3 * P], U8, "r_bytes", "pb_a")
         r_view = r_bytes[:].bitcast(I32).rearrange("p (l t h b r) -> p l t h b r", l=3, t=3, h=2, b=8)
@@ -171,6 +178,10 @@ def tile_picked_mthhzncpsdesntw_none_p_kernel(
         nc.vector.tensor_copy(r_view[:, :, 1:3, 0], d_bytes0[:, :, 2:4])
         nc.vector.tensor_copy(r_view[:, :, 1:3, 1], d_bytes1[:, :, 2:4])
         place_rows(r_plane, r_bytes)
+        w_raw = tile([P, 4, N], F32, "w_raw", "pb_a")
+        w_rows = w1.rearrange("(b s r) n -> s b r n", s=4, r=8)
+        for s in range(4):
+            nc.sync.dma_start(w_raw[:, s, :], w_rows[s])
 
         ub = {}
         ds = {}
@@ -191,9 +202,9 @@ def tile_picked_mthhzncpsdesntw_none_p_kernel(
         put4("a")
         put5("a")
 
-        words1 = [gather_d_words(l, 1, tag) for l, tag in enumerate(("pa_a", "a_codes0"))]
+        words1 = [gather_d_words(l, 1, tag) for l, tag in enumerate(("pa_a", "xw_tab"))]
         b_codes = [deal_pair(words1[0], "b_codes0")]
-        words1.append(gather_d_words(2, 1, "ra_a"))
+        words1.append(gather_d_words(2, 1, "rb_a"))
         b_codes.extend(deal_pair(words1[l], "b_codes%d" % l) for l in (1, 2))
 
         def r_scales(t):
@@ -209,8 +220,8 @@ def tile_picked_mthhzncpsdesntw_none_p_kernel(
         nc.scalar.activation(h_b[:], acc_b[:], ACT.Copy, scale=0.0625)
         pair_b = fetch_pairs(h_b, "b")
         cd_codes = tile([P, 3, 2, P], I32, "cd_codes", "b_codes0")
+        nc.vector.tensor_copy(cd_codes[:, :, :, 0:64].rearrange("p l s (b r) -> p s l b r", b=8), words0[:, 2:4])
         for l in range(3):
-            deal_cd(words0[l], l, 0)
             deal_cd(words1[l], l, 1)
         res["b"] = combine(pair_b, "b")
         h_c = scaled(product([cd_codes[:, l, 0, :] for l in range(3)], r_scales(1), "acc_c"), "c")

@@ -57,6 +57,9 @@ def tile_picked_mthhzncpsdesntw_none_p_kernel(
             load_list(ap, "n%d" % (i + 1)) for i, ap in enumerate((n1, n2, n3, n4, n5, n6, n7, n8))
         ]
 
+        warm = tile([P, 2], F32, "warm")
+        nc.vector.memset(warm[:], 0.0)
+        nc.scalar.activation(warm[:, 1:2], warm[:, 0:1], ACT.Sigmoid)
         first_plane = tile([P, 3 * P + 3 * S], U8, "first_plane")
         a_plane = first_plane[:, : 3 * P]
         x_plane = first_plane[:, 3 * P :]
@@ -240,16 +243,18 @@ def tile_picked_mthhzncpsdesntw_none_p_kernel(
         put5("c")
         put5("d")
 
-        z = tile([P, 4 * S], BF16, "z")
-        z_slots = z[:].rearrange("p (j s) -> p j s", s=4)
+        first_pieces = [(0, 64), (64, W), (W, S)]
+        z = [tile([P, 4 * (j1 - j0)], BF16, "z%d" % j0) for j0, j1 in first_pieces]
+        z_slots = [t[:].rearrange("p (j s) -> p j s", s=4) for t in z]
 
         def difference(name, tag, j0, j1):
             d = tile([P, j1 - j0], F32, "diff_%s%d" % (name, j0), tag)
             nc.vector.tensor_tensor(d[:], ub[name][:, j0:j1], ds[name][:, j0:j1], ALU.subtract)
             return d
 
-        def gain(d, s, j0, j1):
-            nc.vector.tensor_scalar(z_slots[:, j0:j1, s], d[:], cols[:, s, 0:1], None, ALU.mult)
+        def gain(d, s):
+            for u, (j0, j1) in enumerate(first_pieces):
+                nc.vector.tensor_scalar(z_slots[u][:, :, s], d[:, j0:j1], cols[:, s, 0:1], None, ALU.mult)
 
         slot0 = difference("a", "h_c", 0, S)
         slot1 = tile([P, S], F32, "slot1")
@@ -272,19 +277,18 @@ def tile_picked_mthhzncpsdesntw_none_p_kernel(
         diff_b = difference("b", "pb_d", 0, S)
         nc.sync.dma_start(slot0[64:P, :], diff_b[0:64, :])
         nc.sync.dma_start(slot1[64:P, :], diff_b[64:P, :])
-        gain(slot0, 0, 0, S)
-        gain(slot1, 1, 0, S)
-        gain(difference("c", None, 0, S), 2, 0, S)
-        gained = tile([P, S], F32, "gained")
+        gain(slot0, 0)
+        gain(slot1, 1)
+        gain(difference("c", "slot1", 0, S), 2)
+        gained = tile([P, S], F32, "gained", "h_c")
         nc.vector.tensor_scalar(gained[:], ub["d"][:], cols[:, 3, 0:1], None, ALU.mult)
         z_codes = tile([P, S], I32, "z_codes")
         z_scales = tile([P, S], U8, "z_scales")
-        first_pieces = [(0, 64), (64, W), (W, S)]
-        for j0, j1 in first_pieces:
+        for u, (j0, j1) in enumerate(first_pieces):
             nc.vector.scalar_tensor_tensor(
-                z_slots[:, j0:j1, 3], ds["d"][:, j0:j1], neg_gain[:], gained[:, j0:j1], ALU.mult, ALU.add
+                z_slots[u][:, :, 3], ds["d"][:, j0:j1], neg_gain[:], gained[:, j0:j1], ALU.mult, ALU.add
             )
-            nc.vector.quantize_mx(z_codes[:, j0:j1].bitcast(FP8X4), z_scales[:, j0:j1], z[:, 4 * j0 : 4 * j1])
+            nc.vector.quantize_mx(z_codes[:, j0:j1].bitcast(FP8X4), z_scales[:, j0:j1], z[u][:])
 
         def dense(m, j0, j1, tag):
             acc = psum.tile([P, j1 - j0], F32, name="acc2_%d_%d" % (m, j0), tag=tag)

import concourse.mybir as mybir

F32 = mybir.dt.float32
BF16 = mybir.dt.bfloat16
I32 = mybir.dt.int32
U32 = mybir.dt.uint32
U16 = mybir.dt.uint16
U8 = mybir.dt.uint8
FP8X4 = mybir.dt.float8_e4m3fn_x4
ACT = mybir.ActivationFunctionType
ALU = mybir.AluOpType

P = 128
T, G, S, H, N, W = 1024, 2048, 256, 512, 512, 128
HALF = H // 2
WIDE = 2 * S
FLOPS = 2 * 512 * H * S * 3 + 2 * H * N * S


def tile_picked_mthhzncpsdesntw_none_p_kernel(
    tc, x_words, x_scales, d_words, d_scales, gn, w1, sl, th,
    offs, k1, hz, k2, hy, k3, n1, n2, n3, n4, n5, n6, n7, n8, out,
):
    nc = tc.nc
    with (
        tc.tile_pool(name="lists", bufs=1) as lists,
        tc.tile_pool(name="sb", bufs=1) as sb,
        tc.psum_pool(name="psum", bufs=1) as psum,
    ):
        def tile(shape, dtype, name, tag=None):
            return sb.tile(shape, dtype, name=name, tag=tag or name, align_bytes=64)

        def load_list(ap, name):
            t = lists.tile(list(ap.shape), U16, name=name)
            nc.sync.dma_start(t[:], ap)
            return t

        def load_scales(ap, cols, name):
            t = tile([P, cols], U8, name)
            rows = ap[0].bitcast(I32).unsqueeze(1).to_broadcast([16, 8, cols // 4])
            nc.scalar.dma_start(t[:].bitcast(I32), rows)
            return t

        def load_words(ap, cols, name, queue):
            t = tile([P, cols], I32, name)
            queue.dma_start(t[:], ap[0].rearrange("p n t -> p (n t)").bitcast(I32))
            return t

        xs_tab = load_scales(x_scales, T, "xs_tab")
        x_lists = [load_list(offs, "offs")]
        ds_tab = load_scales(d_scales, G, "ds_tab")
        d_lists = [load_list(k1, "k1"), load_list(k2, "k2"), load_list(k3, "k3")]
        x_lists.extend([load_list(hz, "hz"), load_list(hy, "hy")])
        dw_tab = load_words(d_words, G, "dw_tab", nc.sync)
        xw_tab = load_words(x_words, T, "xw_tab", nc.sync)
        l1, l2, l3, l4, l5, l6, l7, l8 = [
            load_list(ap, "n%d" % (i + 1)) for i, ap in enumerate((n1, n2, n3, n4, n5, n6, n7, n8))
        ]

        warm = tile([P, 2], F32, "warm")
        nc.vector.memset(warm[:], 0.0)
        nc.scalar.activation(warm[:, 1:2], warm[:, 0:1], ACT.Sigmoid)
        first_plane = tile([P, 3 * P + 3 * S], U8, "first_plane")
        a_plane = first_plane[:, : 3 * P]
        x_plane = first_plane[:, 3 * P :]
        r_plane = tile([P, 3 * 3 * P], U8, "r_plane")
        for plane in (first_plane, r_plane):
            nc.vector.memset(plane[:].bitcast(I32), 0)

        def place_rows(plane, gathered):
            for r in range(4):
                nc.sync.dma_start(plane[r:P:32, :].bitcast(I32), gathered[8 * r : P : 32, :].bitcast(I32))

        def half_of(lst, half):
            return lst[:, half * HALF // 16 : (half + 1) * HALF // 16]

        def gather_d_bytes(half, tag):
            t = tile([P, 3 * HALF], U8, "d_bytes%d" % half, tag)
            for l in range(3):
                nc.vector.tensor_copy(t[:, l * HALF : (l + 1) * HALF], ds_tab[:].indirect(half_of(d_lists[l], half)))
            return t[:].bitcast(I32).rearrange("p (l b s r) -> p l s b r", l=3, b=8, s=4)

        def gather_d_words(l, half, tag):
            t = tile([P, HALF], I32, "d_words%d_%d" % (half, l), tag)
            nc.vector.tensor_copy(t[:].bitcast(U32), dw_tab[:].bitcast(U32).indirect(half_of(d_lists[l], half)))
            return t[:].rearrange("p (b s r) -> p s b r", b=8, s=4)

        x_bytes = tile([P, 3 * S], U8, "x_bytes")

        def gather_x_bytes(l):
            nc.vector.tensor_copy(x_bytes[:, l * S : (l + 1) * S], xs_tab[:].indirect(x_lists[l][:]))

        gather_x_bytes(0)
        d_bytes0 = gather_d_bytes(0, None)
        first_bytes = tile([P, 3 * P + 3 * S], U8, "first_bytes", "xs_tab")
        gather_x_bytes(1)
        gather_x_bytes(2)
        nc.vector.tensor_copy(
            first_bytes[:, : 3 * P].bitcast(I32).rearrange("p (l s b r) -> p l s b r", l=3, s=2, b=8), d_bytes0[:, :, 0:2]
        )
        nc.vector.tensor_copy(first_bytes[:, 3 * P :].bitcast(I32), x_bytes[:].bitcast(I32))
        place_rows(first_plane, first_bytes)

        cols = tile([P, 6, 8], F32, "cols", "xs_tab")
        gn_rows = gn.rearrange("(b s r) o -> s b r o", s=4, r=8)
        with nc.allow_non_contiguous_dma(reason="one value a partition"):
            for s in range(4):
                nc.sync.dma_start(cols[:, s, 0:1], gn_rows[s])
            nc.sync.dma_start(cols[:, 4, 0:4], sl.rearrange("(m p) o -> p (m o)", p=P))
            nc.sync.dma_start(cols[:, 5, 0:4], th.rearrange("(m p) o -> p (m o)", p=P))
        prod = tile([P, 4], F32, "prod")
        bias = tile([P, 4], F32, "bias")
        nc.gpsimd.tensor_tensor(prod[:], cols[:, 4, 0:4], cols[:, 5, 0:4], ALU.mult)
        nc.gpsimd.tensor_scalar(bias[:], prod[:], -1.0, None, ALU.mult)
        neg_gain = tile([P, 1], F32, "neg_gain")
        nc.gpsimd.tensor_scalar(neg_gain[:], cols[:, 3, 0:1], -1.0, None, ALU.mult)


        def deal_pair(src, name):
            t = tile([P, P], I32, name)
            nc.vector.tensor_copy(t[:].rearrange("p (s b r) -> p s b r", s=2, b=8), src[:, 0:2])
            return t

        def deal_cd(src, l, half):
            dst = cd_codes[:, l, :, 64 * half : 64 * (half + 1)].rearrange("p s (b r) -> p s b r", b=8)
            nc.vector.tensor_copy(dst, src[:, 2:4])

        def product(codes, scales, name):
            acc = psum.tile([P, S], F32, name=name)
            for l in range(3):
                nc.tensor.matmul_mx(
                    acc[:], lhsT=codes[l].bitcast(FP8X4), lhsT_scale=scales[l],
                    rhs=x_codes[:, l * S : (l + 1) * S].bitcast(FP8X4), rhs_scale=x_plane[:, l * S : (l + 1) * S],
                    start=(l == 0), stop=(l == 2),
                )
            return acc

        d_words0 = tile([P, 3 * HALF], I32, "d_words0")
        for l in range(3):
            nc.vector.tensor_copy(
                d_words0[:, l * HALF : (l + 1) * HALF].bitcast(U32),
                dw_tab[:].bitcast(U32).indirect(half_of(d_lists[l], 0)),
            )
        words0 = d_words0[:].rearrange("p (l b s r) -> p s l b r", l=3, b=8, s=4)
        a_codes = tile([P, 3 * P], I32, "a_codes")
        nc.vector.tensor_copy(a_codes[:].rearrange("p (l s b r) -> p s l b r", l=3, s=2, b=8), words0[:, 0:2])
        x_codes = tile([P, 3 * S], I32, "x_codes")
        for l in range(3):
            nc.vector.tensor_copy(
                x_codes[:, l * S : (l + 1) * S].bitcast(U32), xw_tab[:].bitcast(U32).indirect(x_lists[l][:])
            )
        acc_a = product([a_codes[:, l * P : (l + 1) * P] for l in range(3)], [a_plane[:, l * P : (l + 1) * P] for l in range(3)], "acc_a")

        def fetch_pairs(h, name):
            pa = tile([P, W], F32, "pa_" + name)
            pb = tile([P, W], F32, "pb_" + name)
            nc.scalar.activation(pa[:], h[:].indirect(l1[:]), ACT.Copy)
            nc.scalar.activation(pb[:], h[:].indirect(l2[:]), ACT.Copy)
            return pa, pb

        def combine(pair, name):
            pa, pb = pair
            ra = tile([P, W], F32, "ra_" + name)
            rb = tile([P, W], F32, "rb_" + name)
            nc.vector.tensor_tensor(ra[:], pa[:], pb[:], ALU.min)
            nc.vector.tensor_tensor(rb[:], pa[:], pb[:], ALU.add)
            return ra, rb

        def put(window, lst, values):
            nc.scalar.activation(window[:].indirect(lst), values, ACT.Copy)

        h_a = tile([P, S], F32, "h_a")
        nc.scalar.activation(h_a[:], acc_a[:], ACT.Copy, scale=0.0625)
        pair_a = fetch_pairs(h_a, "a")

        d_bytes1 = gather_d_bytes(1, "xw_tab")
        res = {"a": combine(pair_a, "a")}
        r_bytes = tile([P, 3 * 3 * P], U8, "r_bytes", "pb_a")
        r_view = r_bytes[:].bitcast(I32).rearrange("p (l t h b r) -> p l t h b r", l=3, t=3, h=2, b=8)
        nc.vector.tensor_copy(r_view[:, :, 0], d_bytes1[:, :, 0:2])
        nc.vector.tensor_copy(r_view[:, :, 1:3, 0], d_bytes0[:, :, 2:4])
        nc.vector.tensor_copy(r_view[:, :, 1:3, 1], d_bytes1[:, :, 2:4])
        place_rows(r_plane, r_bytes)
        w_raw = tile([P, 4, N], F32, "w_raw", "pb_a")
        w_rows = w1.rearrange("(b s r) n -> s b r n", s=4, r=8)
        for s in range(4):
            nc.sync.dma_start(w_raw[:, s, :], w_rows[s])

        ub = {}
        ds = {}
        for name in "abcd":
            ub[name] = tile([P, S], F32, "ub_" + name)
            ds[name] = tile([P, WIDE], F32, "ds_" + name)

        def put3(name):
            put(ub[name], l3[:], res[name][0][:])

        def put4(name):
            put(ub[name], l4[:], res[name][1][:])

        def put5(name):
            put(ds[name], l5[:], ub[name][:])

        put3("a")
        put4("a")
        put5("a")

        words1 = [gather_d_words(l, 1, tag) for l, tag in enumerate(("pa_a", "xw_tab"))]
        b_codes = [deal_pair(words1[0], "b_codes0")]
        words1.append(gather_d_words(2, 1, "rb_a"))
        b_codes.extend(deal_pair(words1[l], "b_codes%d" % l) for l in (1, 2))

        def r_scales(t):
            return [r_plane[:, (3 * l + t) * P : (3 * l + t + 1) * P] for l in range(3)]

        def scaled(acc, name):
            h = tile([P, S], F32, "h_" + name)
            nc.vector.tensor_scalar(h[:], acc[:], 0.0625, None, ALU.mult)
            return h

        acc_b = product([t[:] for t in b_codes], r_scales(0), "acc_b")
        h_b = tile([P, S], F32, "h_b")
        nc.scalar.activation(h_b[:], acc_b[:], ACT.Copy, scale=0.0625)
        pair_b = fetch_pairs(h_b, "b")
        cd_codes = tile([P, 3, 2, P], I32, "cd_codes", "b_codes0")
        nc.vector.tensor_copy(cd_codes[:, :, :, 0:64].rearrange("p l s (b r) -> p s l b r", b=8), words0[:, 2:4])
        for l in range(3):
            deal_cd(words1[l], l, 1)
        res["b"] = combine(pair_b, "b")
        h_c = scaled(product([cd_codes[:, l, 0, :] for l in range(3)], r_scales(1), "acc_c"), "c")
        h_d = scaled(product([cd_codes[:, l, 1, :] for l in range(3)], r_scales(2), "acc_d"), "d")
        put3("b")
        pair_c = fetch_pairs(h_c, "c")
        put4("b")
        pair_d = fetch_pairs(h_d, "d")
        res["c"] = combine(pair_c, "c")
        res["d"] = combine(pair_d, "d")
        put5("b")
        put3("c")
        put3("d")
        put4("c")
        put4("d")
        put5("c")
        put5("d")

        first_pieces = [(0, 64), (64, W), (W, S)]
        z = [tile([P, 4 * (j1 - j0)], BF16, "z%d" % j0) for j0, j1 in first_pieces]
        z_slots = [t[:].rearrange("p (j s) -> p j s", s=4) for t in z]

        def difference(name, tag, j0, j1):
            d = tile([P, j1 - j0], F32, "diff_%s%d" % (name, j0), tag)
            nc.vector.tensor_tensor(d[:], ub[name][:, j0:j1], ds[name][:, j0:j1], ALU.subtract)
            return d

        def gain(d, s):
            for u, (j0, j1) in enumerate(first_pieces):
                nc.vector.tensor_scalar(z_slots[u][:, :, s], d[:, j0:j1], cols[:, s, 0:1], None, ALU.mult)

        slot0 = difference("a", "h_c", 0, S)
        slot1 = tile([P, S], F32, "slot1")
        nc.sync.dma_start(slot1[0:64, :], slot0[64:P, :])

        w_codes = []
        w_scales = []
        for m, tag in enumerate(("pa_c", "pb_c", "pa_d", "h_d")):
            w_bf = tile([P, 4 * P], BF16, "w_bf%d" % m, tag)
            nc.vector.tensor_copy(
                w_bf[:].rearrange("p (c i s) -> p c s i", i=4, s=4),
                w_raw[:, :, m * P : (m + 1) * P].rearrange("p s (c i) -> p c s i", i=4),
            )
            codes = tile([P, P], I32, "w_codes%d" % m)
            scales = tile([P, P], U8, "w_scales%d" % m)
            nc.vector.quantize_mx(codes[:].bitcast(FP8X4), scales[:], w_bf[:])
            w_codes.append(codes)
            w_scales.append(scales)

        diff_b = difference("b", "pb_d", 0, S)
        nc.sync.dma_start(slot0[64:P, :], diff_b[0:64, :])
        nc.sync.dma_start(slot1[64:P, :], diff_b[64:P, :])
        gain(slot0, 0)
        gain(slot1, 1)
        gain(difference("c", "slot1", 0, S), 2)
        gained = tile([P, S], F32, "gained", "h_c")
        nc.vector.tensor_scalar(gained[:], ub["d"][:], cols[:, 3, 0:1], None, ALU.mult)
        z_codes = tile([P, S], I32, "z_codes")
        z_scales = tile([P, S], U8, "z_scales")
        for u, (j0, j1) in enumerate(first_pieces):
            nc.vector.scalar_tensor_tensor(
                z_slots[u][:, :, 3], ds["d"][:, j0:j1], neg_gain[:], gained[:, j0:j1], ALU.mult, ALU.add
            )
            nc.vector.quantize_mx(z_codes[:, j0:j1].bitcast(FP8X4), z_scales[:, j0:j1], z[u][:])

        def dense(m, j0, j1, tag):
            acc = psum.tile([P, j1 - j0], F32, name="acc2_%d_%d" % (m, j0), tag=tag)
            nc.tensor.matmul_mx(
                acc[:], lhsT=w_codes[m][:].bitcast(FP8X4), lhsT_scale=w_scales[m][:],
                rhs=z_codes[:, j0:j1].bitcast(FP8X4), rhs_scale=z_scales[:, j0:j1], start=True, stop=True,
            )
            return acc

        h2 = []
        first = []
        for u, (j0, j1) in enumerate(first_pieces):
            t = tile([P, j1 - j0], F32, "h2_0_%d" % u)
            acc = dense(0, j0, j1, ("acc_a", "acc_b", "acc2_0")[u])
            if u == 0:
                nc.scalar.copy(t[:], acc[:])
            else:
                nc.vector.tensor_copy(t[:], acc[:])
            first.append((t, j0, j1))
        h2.append(first)
        for m in range(1, 4):
            t = tile([P, S], F32, "h2_%d" % m)
            nc.vector.tensor_copy(t[:], dense(m, 0, S, "acc2_%d" % m)[:])
            h2.append([(t, 0, S)])

        for m in range(4):
            ds2 = tile([P, WIDE], F32, "ds2_%d" % m)
            ds3 = tile([P, WIDE], F32, "ds3_%d" % m)
            for t, j0, j1 in h2[m]:
                put(ds2, l6[:, j0 // 16 : j1 // 16], t[:])
                put(ds3, l7[:, j0 // 16 : j1 // 16], t[:])
            pieces = [(0, W), (W, S)] if m == 3 else [(0, S)]
            for j0, j1 in pieces:
                sg = tile([P, j1 - j0], F32, "sg_%d_%d" % (m, j0))
                nc.scalar.activation(
                    sg[:], ds2[:].indirect(l8[:, j0 // 16 : j1 // 16]), ACT.Sigmoid,
                    scale=cols[:, 4, m : m + 1], bias=bias[:, m : m + 1],
                )
                res_out = tile([P, j1 - j0], F32, "out_%d_%d" % (m, j0))
                nc.vector.tensor_tensor(res_out[:], ds3[:, j0:j1], sg[:], ALU.mult)
                nc.sync.dma_start(out[m * P : (m + 1) * P, j0:j1], res_out[:])
